import numpy as np
import ml_dtypes


def mxq(x, axis, fmt="e4m3"):
    dtype, down = {"e4m3": (ml_dtypes.float8_e4m3fn, 7), "e5m2": (ml_dtypes.float8_e5m2, 14)}[fmt]
    v = np.moveaxis(np.asarray(x, np.float32).astype(ml_dtypes.bfloat16).astype(np.float64), axis, -1)
    blocks = v.reshape(v.shape[:-1] + (-1, 32))
    amax = np.abs(blocks).max(-1, keepdims=True)
    byte = np.maximum(np.where(amax > 0, np.frexp(amax)[1] - 1 + 127, 0) - down, 1)
    scale = np.exp2(byte - 127.0)
    codes = (blocks / scale).astype(np.float32).astype(dtype).astype(np.float64)
    return np.moveaxis((codes * scale).reshape(v.shape), -1, axis)


WIDE = False


def mx_kscale(k):
    if not WIDE:
        return np.ones(k)
    levels = np.array([10, -10, 5, -5, 0])
    if k % 512:
        return np.exp2(np.random.permutation(np.resize(levels, k // 32))).repeat(32)
    a = np.empty((k // 512, 16))
    for p in range(k // 512):
        a[p, :8] = np.random.permutation(np.resize(levels, 8))
        for g in range(8):
            far = levels[np.abs(levels - a[p, g]) >= 10]
            a[p, g + 8] = far[np.random.randint(len(far))]
    return np.exp2(a.ravel()).repeat(32)


BF16 = ml_dtypes.bfloat16


def bf(x):
    return np.asarray(x, np.float32).astype(BF16)


def f64(x):
    return np.asarray(x).astype(np.float64)


Q, N, R, P = 2048, 1024, 512, 1024


def draw0():
    s, u = mx_kscale(N), mx_kscale(Q)
    return {"bx": bf(np.random.standard_normal((Q, N)) * s * u[:, None]),
            "by": bf(np.random.standard_normal((Q, N)) * s * u[:, None]),
            "v": bf(np.random.standard_normal((N, R)) / np.sqrt(N) / s[:, None]),
            "theta": bf(np.random.uniform(-1.5, 1.5, (Q,))),
            "log_along": bf(0.3 + 0.3 * np.random.standard_normal((Q,))),
            "log_across": bf(-0.9 + 0.3 * np.random.standard_normal((Q,))),
            "wq": bf(np.random.uniform(0.5, 1.5, (Q,))),
            "tx": bf(np.random.standard_normal((Q, P)) / np.sqrt(Q) / u[:, None]),
            "ty": bf(np.random.standard_normal((Q, P)) / np.sqrt(Q) / u[:, None])}


def conductivity(theta, log_along, log_across, wq):
    c, d = np.cos(theta), np.sin(theta)
    along, across = wq * np.exp(log_along), wq * np.exp(log_across)
    kxx = along * c * c + across * d * d
    kyy = along * d * d + across * c * c
    kxy = (along - across) * c * d
    return kxx[:, None], kxy[:, None], kyy[:, None]


def core(bx, by, v, theta, log_along, log_across, wq, tx, ty):
    vq = mxq(f64(v), 0, "e4m3")
    gx = mxq(f64(bx), 1, "e4m3") @ vq
    gy = mxq(f64(by), 1, "e4m3") @ vq
    kxx, kxy, kyy = conductivity(f64(theta), f64(log_along), f64(log_across), f64(wq))
    fx = kxx * gx + kxy * gy
    fy = kxy * gx + kyy * gy
    sx = mxq(f64(tx), 0, "e4m3").T @ mxq(fx, 0, "e4m3")
    sy = mxq(f64(ty), 0, "e4m3").T @ mxq(fy, 0, "e4m3")
    return sx + sy


def e4m3fn_bytes(y):
    return np.clip(np.asarray(y, np.float64), -448.0, 448.0).astype(np.float32).astype(ml_dtypes.float8_e4m3fn).view(np.uint8)


def e4m3fn_values(b):
    return np.asarray(b, np.uint8).view(ml_dtypes.float8_e4m3fn).astype(np.float64)


def setup_inputs():
    d = draw0()
    x0 = np.asarray(d['ty']).astype(np.float64)
    s = (np.max(np.abs(x0), axis=(1,), keepdims=True) / 448.0).astype(np.float32)
    out = {}
    for k, v in d.items():
        if k == 'ty':
            out['ty_bytes'] = e4m3fn_bytes(x0 / s.astype(np.float64))
            out['ty_scale'] = s
        else:
            out[k] = v
    return out


def reference(bx, by, v, theta, log_along, log_across, wq, tx, ty_bytes, ty_scale):
    return core(bx, by, v, theta, log_along, log_across, wq, tx, e4m3fn_values(ty_bytes) * ty_scale.astype(np.float64))

@@ -1,0 +1,377 @@
+from contextlib import ExitStack
+
+import concourse.mybir as mybir
+from concourse.masks import make_identity
+
+Q, N, R, P = 2048, 1024, 512, 1024
+FLOPS = 4 * Q * N * R + 4 * Q * P * R
+
+F32 = mybir.dt.float32
+BF16 = mybir.dt.bfloat16
+U32 = mybir.dt.uint32
+U8 = mybir.dt.uint8
+FP8 = mybir.dt.float8_e4m3fn
+FP8X4 = mybir.dt.float8_e4m3fn_x4
+ACT = mybir.ActivationFunctionType
+ALU = mybir.AluOpType
+
+LANES = 128
+GROUPS = Q // 512
+STEPS = Q // 128
+XY_AHEAD = 10
+WIDEN_STEPS = (5, 7, 9, 13, 15)
+SCALAR_TX = (0, 2, 4, 6, 8, 9, 10, 11, 12, 13, 14)
+E_FIRST = True
+T_FIRST = True
+F_LAG = 1
+VECTOR_EMPTY = ((2, 1), (5, 1), (7, 1))
+
+
+def tile_reduced_stiffness_projection_f4_kernel(
+    tc, bx, by, v, theta, log_along, log_across, wq, tx, ty_bytes, ty_scale, out
+):
+    nc = tc.nc
+    with ExitStack() as ctx:
+        keep = ctx.enter_context(tc.tile_pool(name="keep", bufs=1))
+        xyp = ctx.enter_context(tc.tile_pool(name="xyp", bufs=XY_AHEAD))
+        two = ctx.enter_context(tc.tile_pool(name="two", bufs=2))
+        three = ctx.enter_context(tc.tile_pool(name="three", bufs=3))
+        four = ctx.enter_context(tc.tile_pool(name="four", bufs=4))
+        tpool = ctx.enter_context(tc.psum_pool(name="tpool", bufs=4))
+        gpool = ctx.enter_context(tc.psum_pool(name="gpool", bufs=4))
+
+        ident = keep.tile([LANES, 128], F32, name="ident")
+        make_identity(nc, ident[:])
+        rows = keep.tile([LANES, 512], BF16, name="rows")
+        one = keep.tile([LANES, 1], F32, name="one")
+        ctx.enter_context(tc.manual_schedule())
+
+        nc.vector.memset(rows[:], 0.0)
+        nc.vector.memset(one[:], 0.0)
+        for n, vec in enumerate((theta, log_along, log_across, wq)):
+            nc.scalar.dma_start(out=rows[4 * n : 4 * n + 4, :], in_=vec.rearrange("(g c) -> g c", g=4))
+        nc.scalar.activation(out=one[:], in_=one[:], func=ACT.Sin)
+
+        v_raw = []
+        for g in range(2):
+            t = keep.tile([LANES, 4, R], BF16, name=f"v_raw{g}")
+            nc.sync.dma_start(out=t[:], in_=v[512 * g : 512 * g + 512, :].rearrange("(p t) n -> p t n", t=4))
+            v_raw.append(t)
+
+        xy = {}
+        ty_raw = {}
+        tx_raw = {}
+
+        def load_xy(i):
+            g, t = divmod(i, 4)
+            tile = xyp.tile([LANES, 2, N], BF16, name="xy")
+            for side, src in enumerate((bx, by)):
+                nc.sync.dma_start(
+                    out=tile[:, side, :],
+                    in_=src[512 * g : 512 * g + 512, :].rearrange("(m t) k -> m t k", t=4)[:, t, :],
+                )
+            xy[i] = tile
+
+        def load_ty(g):
+            tile = four.tile([LANES, 4, P], U8, name="ty_raw")
+            nc.sync.dma_start(
+                out=tile[:], in_=ty_bytes[512 * g : 512 * g + 512, :].rearrange("(p t) c -> p t c", t=4)
+            )
+            ty_raw[g] = tile
+
+        def load_tx(g):
+            tile = three.tile([LANES, 4, P], BF16, name="tx_raw")
+            nc.sync.dma_start(
+                out=tile[:], in_=tx[512 * g : 512 * g + 512, :].rearrange("(p t) c -> p t c", t=4)
+            )
+            tx_raw[g] = tile
+
+        for i in range(5):
+            load_xy(i)
+        tsc = keep.tile([LANES, 4, 4], F32, name="tsc")
+        nc.sync.dma_start(out=tsc[:], in_=ty_scale.rearrange("(g p t) o -> p g (t o)", p=128, t=4))
+        load_ty(0)
+        for i in range(5, XY_AHEAD):
+            load_xy(i)
+
+        kps = gpool.tile([LANES, 512], F32, name="gbank")
+        words = rows[:].bitcast(F32)
+        for u in range(2):
+            nc.tensor.transpose(kps[:, 128 * u : 128 * u + 128], words[:, u : 256 : 2], ident[:])
+        kview = kps[:, 0:256].bitcast(BF16).rearrange("p (u r e) -> p u r e", u=2, e=2)
+        kin = keep.tile([LANES, 5, 16], F32, name="kin")
+
+        def kslot(tile, n):
+            return tile[:, n, :].rearrange("p (u g e) -> p u g e", u=2, e=2)
+
+        nc.scalar.activation(out=kslot(kin, 0), in_=kview[:, :, 0:4, :], func=ACT.Sin)
+        nc.scalar.activation(out=kslot(kin, 1), in_=kview[:, :, 0:4, :], func=ACT.Sin, scale=0.5)
+        nc.scalar.activation(out=kslot(kin, 2), in_=kview[:, :, 4:8, :], func=ACT.Exp)
+        nc.scalar.activation(out=kslot(kin, 3), in_=kview[:, :, 8:12, :], func=ACT.Exp)
+        nc.scalar.copy(out=kslot(kin, 4), in_=kview[:, :, 12:16, :])
+
+        kk = keep.tile([LANES, 3, 16], F32, name="kk")
+        tmp = keep.tile([LANES, 12, 16], F32, name="tmp")
+
+        def conductivity():
+            def tt(o, a, b, op):
+                nc.vector.tensor_tensor(out=o, in0=a, in1=b, op=op)
+
+            sn, sh = kin[:, 0, :], kin[:, 1, :]
+            h, c, c2, d2, cd = (tmp[:, n, :] for n in range(5))
+            a, b = tmp[:, 5, :], tmp[:, 6, :]
+            nc.vector.scalar_tensor_tensor(out=h, in0=sh, scalar=-2.0, in1=sh, op0=ALU.mult, op1=ALU.mult)
+            tt(d2, sn, sn, ALU.mult)
+            nc.vector.tensor_scalar(out=c, in0=h, scalar1=1.0, scalar2=None, op0=ALU.add)
+            tt(a, kin[:, 2, :], kin[:, 4, :], ALU.mult)
+            tt(b, kin[:, 3, :], kin[:, 4, :], ALU.mult)
+            tt(c2, c, c, ALU.mult)
+            tt(cd, c, sn, ALU.mult)
+            tt(tmp[:, 7, :], a, d2, ALU.mult)
+            tt(tmp[:, 8, :], b, d2, ALU.mult)
+            tt(tmp[:, 9, :], a, c2, ALU.mult)
+            tt(tmp[:, 10, :], b, c2, ALU.mult)
+            tt(tmp[:, 11, :], a, b, ALU.subtract)
+            tt(kk[:, 0, :], tmp[:, 9, :], tmp[:, 8, :], ALU.add)
+            tt(kk[:, 2, :], tmp[:, 10, :], tmp[:, 7, :], ALU.add)
+            tt(kk[:, 1, :], tmp[:, 11, :], cd, ALU.mult)
+
+        def kcol(n, i):
+            g, t = divmod(i, 4)
+            c = 8 * (t // 2) + 2 * g + t % 2
+            return kk[:, n, c : c + 1]
+
+        def interleave(copy, dst, planes):
+            copy(
+                out=dst.rearrange("p (c i t) -> p c t i", i=4, t=4),
+                in_=planes.rearrange("p t (c i) -> p c t i", i=4),
+            )
+
+        def quantize(codes, scales, src):
+            nc.vector.quantize_mx(out=codes.bitcast(FP8X4), scales=scales, in_=src)
+
+        v_codes = keep.tile([LANES, 2, R], U32, name="v_codes", align_bytes=64)
+        v_scales = keep.tile([LANES, 2, R], U8, name="v_scales", align_bytes=64)
+        v_il = []
+        for g in range(2):
+            t = four.tile([LANES, 2048], BF16, name="il2", align_bytes=64)
+            interleave(nc.vector.tensor_copy, t[:], v_raw[g][:])
+            v_il.append(t)
+        for g in range(2):
+            quantize(v_codes[:, g, :], v_scales[:, g, :], v_il[g][:])
+        conductivity()
+
+        tbank, grp, codes1, gbank, ab = {}, {}, {}, {}, {}
+
+        def transposes(i):
+            tbank[i] = []
+            for side in range(2):
+                bank = tpool.tile([LANES, 4, 128], F32, name="tbank")
+                w = xy[i][:, side, :].bitcast(F32)
+                for g in range(2):
+                    for u in range(2):
+                        nc.tensor.transpose(bank[:, 2 * g + u, :], w[:, 256 * g + u : 256 * g + 256 : 2], ident[:])
+                tbank[i].append(bank)
+
+        def empty(i):
+            tile = three.tile([LANES, 2, 1024], BF16, name="grp", align_bytes=64)
+            for side in range(2):
+                copy = nc.vector.tensor_copy if (i, side) in VECTOR_EMPTY else nc.scalar.copy
+                copy(
+                    out=tile[:, side, :].bitcast(F32).rearrange("p (g r u) -> p g r u", g=2, u=2),
+                    in_=tbank[i][side][:].rearrange("p (g u) r -> p g r u", g=2),
+                )
+            grp[i] = tile
+
+        def quant1(i):
+            c = three.tile([LANES, 512], U32, name="codes1", align_bytes=64)
+            s = three.tile([LANES, 512], U8, name="scales1", align_bytes=64)
+            quantize(c[:], s[:], grp[i][:].rearrange("p a b -> p (a b)"))
+            codes1[i] = (c, s)
+
+        def mm1(i):
+            c, s = codes1[i]
+            gbank[i] = []
+            for side in range(2):
+                bank = gpool.tile([LANES, R], F32, name="gbank")
+                for g in range(2):
+                    w = slice(256 * side + 128 * g, 256 * side + 128 * g + 128)
+                    nc.tensor.matmul_mx(
+                        out=bank[:],
+                        lhsT=c[:, w].bitcast(FP8X4),
+                        lhsT_scale=s[:, w],
+                        rhs=v_codes[:, g, :].bitcast(FP8X4),
+                        rhs_scale=v_scales[:, g, :],
+                        start=(g == 0),
+                        stop=(g == 1),
+                    )
+                gbank[i].append(bank)
+
+        def cross(i):
+            a = three.tile([LANES, R], F32, name="cross_x")
+            b = three.tile([LANES, R], F32, name="cross_y")
+            nc.scalar.activation(out=a[:], in_=gbank[i][1][:], func=ACT.Copy, scale=kcol(1, i))
+            nc.scalar.activation(out=b[:], in_=gbank[i][0][:], func=ACT.Copy, scale=kcol(1, i))
+            ab[i] = (a, b)
+
+        flux = {}
+        fcodes = {}
+        fil = {}
+
+        def flux_step(i):
+            g, t = divmod(i, 4)
+            if t == 0:
+                flux[g] = (
+                    two.tile([LANES, 4, R], BF16, name="flux_x"),
+                    two.tile([LANES, 4, R], BF16, name="flux_y"),
+                )
+            for side in range(2):
+                nc.vector.scalar_tensor_tensor(
+                    out=flux[g][side][:, t, :],
+                    in0=gbank[i][side][:],
+                    scalar=kcol(2 * side, i),
+                    in1=ab[i][side][:],
+                    op0=ALU.mult,
+                    op1=ALU.add,
+                )
+
+        def flux_il(g, k):
+            side, half = divmod(k, 2)
+            tile = three.tile([LANES, 1024], BF16, name="fil", align_bytes=64)
+            interleave(nc.vector.tensor_copy, tile[:], flux[g][side][:, :, 256 * half : 256 * half + 256])
+            fil[g, k] = tile
+
+        def flux_q(g, k):
+            side, half = divmod(k, 2)
+            if half == 0:
+                fcodes[g, side] = (
+                    keep.tile([LANES, R], U32, name=f"fc{g}{side}", align_bytes=64),
+                    keep.tile([LANES, R], U8, name=f"fs{g}{side}", align_bytes=64),
+                )
+            c, s = fcodes[g, side]
+            w = slice(256 * half, 256 * half + 256)
+            quantize(c[:, w], s[:, w], fil[g, k][:])
+
+        wide = {}
+
+        def widen(g, t):
+            if t == 0:
+                wide[g] = three.tile([LANES, 4, P], BF16, name="wide")
+            nc.scalar.activation(
+                out=wide[g][:, t, :], in_=ty_raw[g][:, t, :].bitcast(FP8), func=ACT.Copy, scale=tsc[:, g, t : t + 1]
+            )
+
+        widen_todo = [(g, t) for g in range(4) for t in range(4)]
+
+        transposes(0)
+        transposes(1)
+        empty(0)
+        later = {0: ("ty", 1), 2: ("tx", 0), 4: ("ty", 2), 5: ("ty", 3), 6: ("tx", 1), 7: ("tx", 2)}
+        for i in range(STEPS):
+            if i + XY_AHEAD < STEPS:
+                load_xy(i + XY_AHEAD)
+            if i in later:
+                kind, g = later[i]
+                if kind == "ty":
+                    load_ty(g)
+                else:
+                    load_tx(g)
+            quant1(i)
+            if T_FIRST and i + 2 < STEPS:
+                transposes(i + 2)
+            if F_LAG == 2 and i >= 2:
+                flux_step(i - 2)
+            mm1(i)
+            if E_FIRST and i + 1 < STEPS:
+                empty(i + 1)
+            if i >= 1:
+                cross(i - 1)
+            if not E_FIRST and i + 1 < STEPS:
+                empty(i + 1)
+            if not T_FIRST and i + 2 < STEPS:
+                transposes(i + 2)
+            g, k = divmod(i - 4 - F_LAG, 4)
+            if g >= 0:
+                flux_il(g, k)
+            if F_LAG == 1 and i >= 1:
+                flux_step(i - 1)
+            if g >= 0:
+                flux_q(g, k)
+            if i in WIDEN_STEPS:
+                widen(*widen_todo.pop(0))
+        if F_LAG == 2:
+            flux_step(STEPS - 2)
+        cross(STEPS - 1)
+
+        il2, codes2, obank = {}, {}, {}
+
+        def il_slice(j, side):
+            g, s = divmod(j, 4)
+            if j not in il2:
+                il2[j] = four.tile([LANES, 2048], BF16, name="il2", align_bytes=64)
+            src = tx_raw[g] if side == 0 else wide[g]
+            copy = nc.scalar.copy if (side == 0 and j in SCALAR_TX) else nc.vector.tensor_copy
+            interleave(copy, il2[j][:, 1024 * side : 1024 * side + 1024], src[:, :, 256 * s : 256 * s + 256])
+
+        def quant2(j):
+            c = four.tile([LANES, 512], U32, name="codes2", align_bytes=64)
+            s = four.tile([LANES, 512], U8, name="scales2", align_bytes=64)
+            quantize(c[:], s[:], il2[j][:])
+            codes2[j] = (c, s)
+
+        def mm2(j):
+            g, s = divmod(j, 4)
+            c, sc = codes2[j]
+            for h in range(2):
+                p = 2 * s + h
+                if g == 0:
+                    if p < 4:
+                        obank[p] = tpool.tile([LANES, R], F32, name="tbank")
+                    else:
+                        obank[p] = gpool.tile([LANES, R], F32, name="gbank")
+                for side in range(2):
+                    w = slice(256 * side + 128 * h, 256 * side + 128 * h + 128)
+                    fc, fs = fcodes[g, side]
+                    nc.tensor.matmul_mx(
+                        out=obank[p][:],
+                        lhsT=c[:, w].bitcast(FP8X4),
+                        lhsT_scale=sc[:, w],
+                        rhs=fc[:].bitcast(FP8X4),
+                        rhs_scale=fs[:],
+                        start=(g == 0 and side == 0),
+                        stop=(g == 3 and side == 1),
+                    )
+
+        def finish(p):
+            t = four.tile([LANES, R], F32, name="res", bufs=6)
+            if p == 7:
+                nc.vector.tensor_copy(out=t[:], in_=obank[p][:])
+            else:
+                nc.scalar.copy(out=t[:], in_=obank[p][:])
+            nc.sync.dma_start(out=out[128 * p : 128 * p + 128, :], in_=t[:])
+
+        late_flux = [(2, 3), (3, 0), (3, 1), (3, 2), (3, 3)] if F_LAG == 1 else [(2, 2), (2, 3), (3, 0), (3, 1), (3, 2), (3, 3)]
+        widen(*widen_todo.pop(0))
+        il_slice(0, 0)
+        flux_step(STEPS - 1)
+        for j in range(17):
+            if j < 16:
+                il_slice(j, 1)
+                if j not in SCALAR_TX:
+                    il_slice(j, 0)
+                if j < len(late_flux):
+                    flux_il(*late_flux[j])
+            if j + 1 < 16 and j + 1 in SCALAR_TX:
+                il_slice(j + 1, 0)
+            if j < 11 and widen_todo:
+                widen(*widen_todo.pop(0))
+            if j >= 1:
+                quant2(j - 1)
+                mm2(j - 1)
+            if j < len(late_flux):
+                flux_q(*late_flux[j])
+            if j == 3:
+                load_tx(3)
+            if j - 1 >= 12:
+                finish(2 * (j - 13))
+                finish(2 * (j - 13) + 1)

@@ -18,13 +18,19 @@ ALU = mybir.AluOpType
 LANES = 128
 GROUPS = Q // 512
 STEPS = Q // 128
-XY_AHEAD = 10
-WIDEN_STEPS = (5, 7, 9, 13, 15)
-SCALAR_TX = (0, 2, 4, 6, 8, 9, 10, 11, 12, 13, 14)
-E_FIRST = True
-T_FIRST = True
-F_LAG = 1
-VECTOR_EMPTY = ((2, 1), (5, 1), (7, 1))
+XY_AHEAD = 8
+WIDEN_STEPS = (3, 5, 9, 13, 15)
+VECTOR_EMPTY = ((2, 0), (2, 1), (5, 1), (11, 1))
+PE_STEPS = (5, 6, 7, 8, 9, 10, 11, 13, 14)
+TX_POOL = ((0, 0), (0, 1), (1, 0), (2, 1))
+POOL_START = 4
+SCALAR_TY = (0, 6, 9, 11)
+VECTOR_WIDEN = (0, 14)
+VECTOR_OUT = (6,)
+POOL_WIDTH = 128
+LATE_W = 11
+TX3_STEP = 7
+EARLY_W = 1
 
 
 def tile_reduced_stiffness_projection_f4_kernel(
@@ -42,6 +48,8 @@ def tile_reduced_stiffness_projection_f4_kernel(
 
         ident = keep.tile([LANES, 128], F32, name="ident")
         make_identity(nc, ident[:])
+        ident_bf = keep.tile([LANES, 128], BF16, name="ident_bf")
+        make_identity(nc, ident_bf[:])
         rows = keep.tile([LANES, 512], BF16, name="rows")
         one = keep.tile([LANES, 1], F32, name="one")
         ctx.enter_context(tc.manual_schedule())
@@ -80,7 +88,7 @@ def tile_reduced_stiffness_projection_f4_kernel(
             ty_raw[g] = tile
 
         def load_tx(g):
-            tile = three.tile([LANES, 4, P], BF16, name="tx_raw")
+            tile = four.tile([LANES, 4, P], BF16, name="tx_raw")
             nc.sync.dma_start(
                 out=tile[:], in_=tx[512 * g : 512 * g + 512, :].rearrange("(p t) c -> p t c", t=4)
             )
@@ -152,13 +160,12 @@ def tile_reduced_stiffness_projection_f4_kernel(
 
         v_codes = keep.tile([LANES, 2, R], U32, name="v_codes", align_bytes=64)
         v_scales = keep.tile([LANES, 2, R], U8, name="v_scales", align_bytes=64)
-        v_il = []
+        v_il = three.tile([LANES, 4, P], BF16, name="wide", align_bytes=64)
+        v_flat = v_il[:].rearrange("p t c -> p (t c)")
         for g in range(2):
-            t = four.tile([LANES, 2048], BF16, name="il2", align_bytes=64)
-            interleave(nc.vector.tensor_copy, t[:], v_raw[g][:])
-            v_il.append(t)
+            interleave(nc.vector.tensor_copy, v_flat[:, 2048 * g : 2048 * g + 2048], v_raw[g][:])
         for g in range(2):
-            quantize(v_codes[:, g, :], v_scales[:, g, :], v_il[g][:])
+            quantize(v_codes[:, g, :], v_scales[:, g, :], v_flat[:, 2048 * g : 2048 * g + 2048])
         conductivity()
 
         tbank, grp, codes1, gbank, ab = {}, {}, {}, {}, {}
@@ -256,72 +263,136 @@ def tile_reduced_stiffness_projection_f4_kernel(
 
         def widen(g, t):
             if t == 0:
-                wide[g] = three.tile([LANES, 4, P], BF16, name="wide")
+                wide[g] = three.tile([LANES, 4, P], BF16, name="wide", align_bytes=64)
+            if 4 * g + t in VECTOR_WIDEN:
+                nc.vector.tensor_scalar(
+                    out=wide[g][:, t, :],
+                    in0=ty_raw[g][:, t, :].bitcast(FP8),
+                    scalar1=tsc[:, g, t : t + 1],
+                    scalar2=None,
+                    op0=ALU.mult,
+                )
+                return
             nc.scalar.activation(
                 out=wide[g][:, t, :], in_=ty_raw[g][:, t, :].bitcast(FP8), func=ACT.Copy, scale=tsc[:, g, t : t + 1]
             )
 
         widen_todo = [(g, t) for g in range(4) for t in range(4)]
 
+        tx_codes = [keep.tile([LANES, P], U32, name=f"txc{g}", align_bytes=64) for g in range(4)]
+        tx_scales = [keep.tile([LANES, P], U8, name=f"txs{g}", align_bytes=64) for g in range(4)]
+        tx_bank, tx_il = {}, {}
+
+        def tx_identity(g, s):
+            bank = tpool.tile([LANES, 1024], BF16, name="tbank")
+            for h in range(2):
+                nc.tensor.matmul(
+                    bank[:, 512 * h : 512 * h + 512],
+                    ident_bf[:],
+                    tx_raw[g][:, :, 256 * s + 128 * h : 256 * s + 128 * h + 128].rearrange("p t c -> p c t"),
+                    start=True,
+                    stop=True,
+                )
+            tx_bank[g, s] = bank
+
+        def tx_empty(g, s):
+            tile = three.tile([LANES, 1024], BF16, name="tx_il", align_bytes=64)
+            nc.scalar.copy(out=tile[:], in_=tx_bank[g, s][:])
+            tx_il[g, s] = tile
+
+        def tx_direct(copy, g, s):
+            tile = three.tile([LANES, 1024], BF16, name="tx_il", align_bytes=64)
+            interleave(copy, tile[:], tx_raw[g][:, :, 256 * s : 256 * s + 256])
+            tx_il[g, s] = tile
+
+        def tx_quant(g, s):
+            w = slice(256 * s, 256 * s + 256)
+            quantize(tx_codes[g][:, w], tx_scales[g][:, w], tx_il[g, s][:])
+
+        pool_todo = [(g, 256 * s + c, POOL_WIDTH) for g, s in TX_POOL for c in range(0, 256, POOL_WIDTH)]
+        pool_ready = []
+
+        def pool_il():
+            g, c, n = pool_todo.pop(0)
+            tile = keep.tile([LANES, 4 * POOL_WIDTH], BF16, name="gate", align_bytes=64)
+            nc.gpsimd.tensor_scalar(
+                out=tile[:].rearrange("p (c t) -> p c t", t=4),
+                in0=tx_raw[g][:, :, c : c + n].rearrange("p t c -> p c t"),
+                scalar1=1.0,
+                scalar2=0.0,
+                op0=ALU.mult,
+                op1=ALU.add,
+            )
+            pool_ready.append((g, c, n, tile))
+
+        def pool_quant():
+            g, c, n, tile = pool_ready.pop(0)
+            quantize(tx_codes[g][:, c : c + n], tx_scales[g][:, c : c + n], tile[:])
+
         transposes(0)
         transposes(1)
         empty(0)
-        later = {0: ("ty", 1), 2: ("tx", 0), 4: ("ty", 2), 5: ("ty", 3), 6: ("tx", 1), 7: ("tx", 2)}
+        later = {0: [("tx", 0)], 1: [("ty", 1)], 2: [("tx", 1)], 3: [("tx", 2)], 4: [("ty", 2)], 5: [("ty", 3)]}
+        pe_tx = dict(zip(PE_STEPS, [(g, s) for g in range(4) for s in range(4) if (g, s) not in TX_POOL]))
+        quant_due = []
         for i in range(STEPS):
             if i + XY_AHEAD < STEPS:
                 load_xy(i + XY_AHEAD)
-            if i in later:
-                kind, g = later[i]
+            for kind, g in later.get(i, ()):
                 if kind == "ty":
                     load_ty(g)
                 else:
                     load_tx(g)
+            if i == TX3_STEP:
+                load_tx(3)
             quant1(i)
-            if T_FIRST and i + 2 < STEPS:
+            if i + 2 < STEPS:
                 transposes(i + 2)
-            if F_LAG == 2 and i >= 2:
-                flux_step(i - 2)
             mm1(i)
-            if E_FIRST and i + 1 < STEPS:
+            if i in pe_tx:
+                tx_identity(*pe_tx[i])
+            if i + 1 < STEPS:
                 empty(i + 1)
             if i >= 1:
                 cross(i - 1)
-            if not E_FIRST and i + 1 < STEPS:
-                empty(i + 1)
-            if not T_FIRST and i + 2 < STEPS:
-                transposes(i + 2)
-            g, k = divmod(i - 4 - F_LAG, 4)
+            if i - 1 in pe_tx:
+                tx_empty(*pe_tx[i - 1])
+                quant_due.append(pe_tx[i - 1])
+            g, k = divmod(i - 5, 4)
             if g >= 0:
                 flux_il(g, k)
-            if F_LAG == 1 and i >= 1:
+            if pool_ready:
+                pool_quant()
+            if i >= POOL_START and pool_todo:
+                pool_il()
+            if i >= 1:
                 flux_step(i - 1)
             if g >= 0:
                 flux_q(g, k)
+            if len(quant_due) > 1:
+                tx_quant(*quant_due.pop(0))
             if i in WIDEN_STEPS:
                 widen(*widen_todo.pop(0))
-        if F_LAG == 2:
-            flux_step(STEPS - 2)
+        if pool_ready:
+            pool_quant()
         cross(STEPS - 1)
 
-        il2, codes2, obank = {}, {}, {}
+        ty_il, codes2, obank = {}, {}, {}
 
-        def il_slice(j, side):
+        def il_slice(j):
             g, s = divmod(j, 4)
-            if j not in il2:
-                il2[j] = four.tile([LANES, 2048], BF16, name="il2", align_bytes=64)
-            src = tx_raw[g] if side == 0 else wide[g]
-            copy = nc.scalar.copy if (side == 0 and j in SCALAR_TX) else nc.vector.tensor_copy
-            interleave(copy, il2[j][:, 1024 * side : 1024 * side + 1024], src[:, :, 256 * s : 256 * s + 256])
+            ty_il[j] = four.tile([LANES, 1024], BF16, name="ty_il", align_bytes=64)
+            copy = nc.scalar.copy if j in SCALAR_TY else nc.vector.tensor_copy
+            interleave(copy, ty_il[j][:], wide[g][:, :, 256 * s : 256 * s + 256])
 
         def quant2(j):
-            c = four.tile([LANES, 512], U32, name="codes2", align_bytes=64)
-            s = four.tile([LANES, 512], U8, name="scales2", align_bytes=64)
-            quantize(c[:], s[:], il2[j][:])
+            c = four.tile([LANES, 256], U32, name="codes2", align_bytes=64)
+            s = four.tile([LANES, 256], U8, name="scales2", align_bytes=64)
+            quantize(c[:], s[:], ty_il[j][:])
             codes2[j] = (c, s)
 
         def mm2(j):
             g, s = divmod(j, 4)
-            c, sc = codes2[j]
             for h in range(2):
                 p = 2 * s + h
                 if g == 0:
@@ -330,7 +401,8 @@ def tile_reduced_stiffness_projection_f4_kernel(
                     else:
                         obank[p] = gpool.tile([LANES, R], F32, name="gbank")
                 for side in range(2):
-                    w = slice(256 * side + 128 * h, 256 * side + 128 * h + 128)
+                    c, sc = (tx_codes[g], tx_scales[g]) if side == 0 else codes2[j]
+                    w = slice(128 * p, 128 * p + 128) if side == 0 else slice(128 * h, 128 * h + 128)
                     fc, fs = fcodes[g, side]
                     nc.tensor.matmul_mx(
                         out=obank[p][:],
@@ -342,36 +414,54 @@ def tile_reduced_stiffness_projection_f4_kernel(
                         stop=(g == 3 and side == 1),
                     )
 
-        def finish(p):
-            t = four.tile([LANES, R], F32, name="res", bufs=6)
-            if p == 7:
-                nc.vector.tensor_copy(out=t[:], in_=obank[p][:])
-            else:
-                nc.scalar.copy(out=t[:], in_=obank[p][:])
-            nc.sync.dma_start(out=out[128 * p : 128 * p + 128, :], in_=t[:])
+        res = {}
 
-        late_flux = [(2, 3), (3, 0), (3, 1), (3, 2), (3, 3)] if F_LAG == 1 else [(2, 2), (2, 3), (3, 0), (3, 1), (3, 2), (3, 3)]
-        widen(*widen_todo.pop(0))
-        il_slice(0, 0)
+        def finish(p):
+            if p % 2 == 0:
+                res[p // 2] = xyp.tile([LANES, 2, R], F32, name="xy")
+            t = res[p // 2]
+            if p in VECTOR_OUT:
+                nc.vector.tensor_copy(out=t[:, p % 2, :], in_=obank[p][:])
+            else:
+                nc.scalar.copy(out=t[:, p % 2, :], in_=obank[p][:])
+            nc.sync.dma_start(out=out[128 * p : 128 * p + 128, :], in_=t[:, p % 2, :])
+
+        late_flux = [(2, 3), (3, 0), (3, 1), (3, 2), (3, 3)]
+        for n in range(EARLY_W):
+            widen(*widen_todo.pop(0))
+        if 0 in SCALAR_TY:
+            il_slice(0)
         flux_step(STEPS - 1)
-        for j in range(17):
+        direct = [(g, s) for g in range(4) for s in range(4) if (g, s) not in TX_POOL and (g, s) not in pe_tx.values()]
+        slots = 17
+        for j in range(slots):
+            if quant_due:
+                tx_quant(*quant_due.pop(0))
+            if j == 0 and 0 not in SCALAR_TY:
+                il_slice(0)
+            elif j < 16 and j not in SCALAR_TY:
+                il_slice(j)
+            if j + 1 < 16 and j + 1 in SCALAR_TY:
+                il_slice(j + 1)
             if j < 16:
-                il_slice(j, 1)
-                if j not in SCALAR_TX:
-                    il_slice(j, 0)
+                if (j // 4, j % 4) in direct:
+                    tx_direct(nc.vector.tensor_copy, j // 4, j % 4)
                 if j < len(late_flux):
                     flux_il(*late_flux[j])
-            if j + 1 < 16 and j + 1 in SCALAR_TX:
-                il_slice(j + 1, 0)
-            if j < 11 and widen_todo:
+            if pool_todo or pool_ready:
+                if pool_ready:
+                    pool_quant()
+                if pool_todo:
+                    pool_il()
+            if j < LATE_W and widen_todo:
                 widen(*widen_todo.pop(0))
             if j >= 1:
                 quant2(j - 1)
+                if ((j - 1) // 4, (j - 1) % 4) in direct:
+                    tx_quant((j - 1) // 4, (j - 1) % 4)
                 mm2(j - 1)
             if j < len(late_flux):
                 flux_q(*late_flux[j])
-            if j == 3:
-                load_tx(3)
             if j - 1 >= 12:
                 finish(2 * (j - 13))
                 finish(2 * (j - 13) + 1)

from contextlib import ExitStack

import concourse.mybir as mybir
from concourse.masks import make_identity

Q, N, R, P = 2048, 1024, 512, 1024
FLOPS = 4 * Q * N * R + 4 * Q * P * R

F32 = mybir.dt.float32
BF16 = mybir.dt.bfloat16
U32 = mybir.dt.uint32
U8 = mybir.dt.uint8
FP8 = mybir.dt.float8_e4m3fn
FP8X4 = mybir.dt.float8_e4m3fn_x4
ACT = mybir.ActivationFunctionType
ALU = mybir.AluOpType

LANES = 128
GROUPS = Q // 512
STEPS = Q // 128
XY_AHEAD = 8
WIDEN_STEPS = (3, 5, 9, 13, 15)
VECTOR_EMPTY = ((2, 0), (2, 1), (5, 1), (11, 1))
PE_STEPS = (5, 6, 7, 8, 9, 10, 11, 13, 14)
TX_POOL = ((0, 0), (0, 1), (1, 0), (2, 1))
POOL_START = 4
SCALAR_TY = (0, 6, 9, 11)
VECTOR_WIDEN = (0, 14)
VECTOR_OUT = (6,)
POOL_WIDTH = 128
LATE_W = 11
TX3_STEP = 7
EARLY_W = 1


def tile_reduced_stiffness_projection_f4_kernel(
    tc, bx, by, v, theta, log_along, log_across, wq, tx, ty_bytes, ty_scale, out
):
    nc = tc.nc
    with ExitStack() as ctx:
        keep = ctx.enter_context(tc.tile_pool(name="keep", bufs=1))
        xyp = ctx.enter_context(tc.tile_pool(name="xyp", bufs=XY_AHEAD))
        two = ctx.enter_context(tc.tile_pool(name="two", bufs=2))
        three = ctx.enter_context(tc.tile_pool(name="three", bufs=3))
        four = ctx.enter_context(tc.tile_pool(name="four", bufs=4))
        tpool = ctx.enter_context(tc.psum_pool(name="tpool", bufs=4))
        gpool = ctx.enter_context(tc.psum_pool(name="gpool", bufs=4))

        ident = keep.tile([LANES, 128], F32, name="ident")
        make_identity(nc, ident[:])
        ident_bf = keep.tile([LANES, 128], BF16, name="ident_bf")
        make_identity(nc, ident_bf[:])
        rows = keep.tile([LANES, 512], BF16, name="rows")
        one = keep.tile([LANES, 1], F32, name="one")
        ctx.enter_context(tc.manual_schedule())

        nc.vector.memset(rows[:], 0.0)
        nc.vector.memset(one[:], 0.0)
        for n, vec in enumerate((theta, log_along, log_across, wq)):
            nc.scalar.dma_start(out=rows[4 * n : 4 * n + 4, :], in_=vec.rearrange("(g c) -> g c", g=4))
        nc.scalar.activation(out=one[:], in_=one[:], func=ACT.Sin)

        v_raw = []
        for g in range(2):
            t = keep.tile([LANES, 4, R], BF16, name=f"v_raw{g}")
            nc.sync.dma_start(out=t[:], in_=v[512 * g : 512 * g + 512, :].rearrange("(p t) n -> p t n", t=4))
            v_raw.append(t)

        xy = {}
        ty_raw = {}
        tx_raw = {}

        def load_xy(i):
            g, t = divmod(i, 4)
            tile = xyp.tile([LANES, 2, N], BF16, name="xy")
            for side, src in enumerate((bx, by)):
                nc.sync.dma_start(
                    out=tile[:, side, :],
                    in_=src[512 * g : 512 * g + 512, :].rearrange("(m t) k -> m t k", t=4)[:, t, :],
                )
            xy[i] = tile

        def load_ty(g):
            tile = four.tile([LANES, 4, P], U8, name="ty_raw")
            nc.sync.dma_start(
                out=tile[:], in_=ty_bytes[512 * g : 512 * g + 512, :].rearrange("(p t) c -> p t c", t=4)
            )
            ty_raw[g] = tile

        def load_tx(g):
            tile = four.tile([LANES, 4, P], BF16, name="tx_raw")
            nc.sync.dma_start(
                out=tile[:], in_=tx[512 * g : 512 * g + 512, :].rearrange("(p t) c -> p t c", t=4)
            )
            tx_raw[g] = tile

        for i in range(5):
            load_xy(i)
        tsc = keep.tile([LANES, 4, 4], F32, name="tsc")
        nc.sync.dma_start(out=tsc[:], in_=ty_scale.rearrange("(g p t) o -> p g (t o)", p=128, t=4))
        load_ty(0)
        for i in range(5, XY_AHEAD):
            load_xy(i)

        kps = gpool.tile([LANES, 512], F32, name="gbank")
        words = rows[:].bitcast(F32)
        for u in range(2):
            nc.tensor.transpose(kps[:, 128 * u : 128 * u + 128], words[:, u : 256 : 2], ident[:])
        kview = kps[:, 0:256].bitcast(BF16).rearrange("p (u r e) -> p u r e", u=2, e=2)
        kin = keep.tile([LANES, 5, 16], F32, name="kin")

        def kslot(tile, n):
            return tile[:, n, :].rearrange("p (u g e) -> p u g e", u=2, e=2)

        nc.scalar.activation(out=kslot(kin, 0), in_=kview[:, :, 0:4, :], func=ACT.Sin)
        nc.scalar.activation(out=kslot(kin, 1), in_=kview[:, :, 0:4, :], func=ACT.Sin, scale=0.5)
        nc.scalar.activation(out=kslot(kin, 2), in_=kview[:, :, 4:8, :], func=ACT.Exp)
        nc.scalar.activation(out=kslot(kin, 3), in_=kview[:, :, 8:12, :], func=ACT.Exp)
        nc.scalar.copy(out=kslot(kin, 4), in_=kview[:, :, 12:16, :])

        kk = keep.tile([LANES, 3, 16], F32, name="kk")
        tmp = keep.tile([LANES, 12, 16], F32, name="tmp")

        def conductivity():
            def tt(o, a, b, op):
                nc.vector.tensor_tensor(out=o, in0=a, in1=b, op=op)

            sn, sh = kin[:, 0, :], kin[:, 1, :]
            h, c, c2, d2, cd = (tmp[:, n, :] for n in range(5))
            a, b = tmp[:, 5, :], tmp[:, 6, :]
            nc.vector.scalar_tensor_tensor(out=h, in0=sh, scalar=-2.0, in1=sh, op0=ALU.mult, op1=ALU.mult)
            tt(d2, sn, sn, ALU.mult)
            nc.vector.tensor_scalar(out=c, in0=h, scalar1=1.0, scalar2=None, op0=ALU.add)
            tt(a, kin[:, 2, :], kin[:, 4, :], ALU.mult)
            tt(b, kin[:, 3, :], kin[:, 4, :], ALU.mult)
            tt(c2, c, c, ALU.mult)
            tt(cd, c, sn, ALU.mult)
            tt(tmp[:, 7, :], a, d2, ALU.mult)
            tt(tmp[:, 8, :], b, d2, ALU.mult)
            tt(tmp[:, 9, :], a, c2, ALU.mult)
            tt(tmp[:, 10, :], b, c2, ALU.mult)
            tt(tmp[:, 11, :], a, b, ALU.subtract)
            tt(kk[:, 0, :], tmp[:, 9, :], tmp[:, 8, :], ALU.add)
            tt(kk[:, 2, :], tmp[:, 10, :], tmp[:, 7, :], ALU.add)
            tt(kk[:, 1, :], tmp[:, 11, :], cd, ALU.mult)

        def kcol(n, i):
            g, t = divmod(i, 4)
            c = 8 * (t // 2) + 2 * g + t % 2
            return kk[:, n, c : c + 1]

        def interleave(copy, dst, planes):
            copy(
                out=dst.rearrange("p (c i t) -> p c t i", i=4, t=4),
                in_=planes.rearrange("p t (c i) -> p c t i", i=4),
            )

        def quantize(codes, scales, src):
            nc.vector.quantize_mx(out=codes.bitcast(FP8X4), scales=scales, in_=src)

        v_codes = keep.tile([LANES, 2, R], U32, name="v_codes", align_bytes=64)
        v_scales = keep.tile([LANES, 2, R], U8, name="v_scales", align_bytes=64)
        v_il = three.tile([LANES, 4, P], BF16, name="wide", align_bytes=64)
        v_flat = v_il[:].rearrange("p t c -> p (t c)")
        for g in range(2):
            interleave(nc.vector.tensor_copy, v_flat[:, 2048 * g : 2048 * g + 2048], v_raw[g][:])
        for g in range(2):
            quantize(v_codes[:, g, :], v_scales[:, g, :], v_flat[:, 2048 * g : 2048 * g + 2048])
        conductivity()

        tbank, grp, codes1, gbank, ab = {}, {}, {}, {}, {}

        def transposes(i):
            tbank[i] = []
            for side in range(2):
                bank = tpool.tile([LANES, 4, 128], F32, name="tbank")
                w = xy[i][:, side, :].bitcast(F32)
                for g in range(2):
                    for u in range(2):
                        nc.tensor.transpose(bank[:, 2 * g + u, :], w[:, 256 * g + u : 256 * g + 256 : 2], ident[:])
                tbank[i].append(bank)

        def empty(i):
            tile = three.tile([LANES, 2, 1024], BF16, name="grp", align_bytes=64)
            for side in range(2):
                copy = nc.vector.tensor_copy if (i, side) in VECTOR_EMPTY else nc.scalar.copy
                copy(
                    out=tile[:, side, :].bitcast(F32).rearrange("p (g r u) -> p g r u", g=2, u=2),
                    in_=tbank[i][side][:].rearrange("p (g u) r -> p g r u", g=2),
                )
            grp[i] = tile

        def quant1(i):
            c = three.tile([LANES, 512], U32, name="codes1", align_bytes=64)
            s = three.tile([LANES, 512], U8, name="scales1", align_bytes=64)
            quantize(c[:], s[:], grp[i][:].rearrange("p a b -> p (a b)"))
            codes1[i] = (c, s)

        def mm1(i):
            c, s = codes1[i]
            gbank[i] = []
            for side in range(2):
                bank = gpool.tile([LANES, R], F32, name="gbank")
                for g in range(2):
                    w = slice(256 * side + 128 * g, 256 * side + 128 * g + 128)
                    nc.tensor.matmul_mx(
                        out=bank[:],
                        lhsT=c[:, w].bitcast(FP8X4),
                        lhsT_scale=s[:, w],
                        rhs=v_codes[:, g, :].bitcast(FP8X4),
                        rhs_scale=v_scales[:, g, :],
                        start=(g == 0),
                        stop=(g == 1),
                    )
                gbank[i].append(bank)

        def cross(i):
            a = three.tile([LANES, R], F32, name="cross_x")
            b = three.tile([LANES, R], F32, name="cross_y")
            nc.scalar.activation(out=a[:], in_=gbank[i][1][:], func=ACT.Copy, scale=kcol(1, i))
            nc.scalar.activation(out=b[:], in_=gbank[i][0][:], func=ACT.Copy, scale=kcol(1, i))
            ab[i] = (a, b)

        flux = {}
        fcodes = {}
        fil = {}

        def flux_step(i):
            g, t = divmod(i, 4)
            if t == 0:
                flux[g] = (
                    two.tile([LANES, 4, R], BF16, name="flux_x"),
                    two.tile([LANES, 4, R], BF16, name="flux_y"),
                )
            for side in range(2):
                nc.vector.scalar_tensor_tensor(
                    out=flux[g][side][:, t, :],
                    in0=gbank[i][side][:],
                    scalar=kcol(2 * side, i),
                    in1=ab[i][side][:],
                    op0=ALU.mult,
                    op1=ALU.add,
                )

        def flux_il(g, k):
            side, half = divmod(k, 2)
            tile = three.tile([LANES, 1024], BF16, name="fil", align_bytes=64)
            interleave(nc.vector.tensor_copy, tile[:], flux[g][side][:, :, 256 * half : 256 * half + 256])
            fil[g, k] = tile

        def flux_q(g, k):
            side, half = divmod(k, 2)
            if half == 0:
                fcodes[g, side] = (
                    keep.tile([LANES, R], U32, name=f"fc{g}{side}", align_bytes=64),
                    keep.tile([LANES, R], U8, name=f"fs{g}{side}", align_bytes=64),
                )
            c, s = fcodes[g, side]
            w = slice(256 * half, 256 * half + 256)
            quantize(c[:, w], s[:, w], fil[g, k][:])

        wide = {}

        def widen(g, t):
            if t == 0:
                wide[g] = three.tile([LANES, 4, P], BF16, name="wide", align_bytes=64)
            if 4 * g + t in VECTOR_WIDEN:
                nc.vector.tensor_scalar(
                    out=wide[g][:, t, :],
                    in0=ty_raw[g][:, t, :].bitcast(FP8),
                    scalar1=tsc[:, g, t : t + 1],
                    scalar2=None,
                    op0=ALU.mult,
                )
                return
            nc.scalar.activation(
                out=wide[g][:, t, :], in_=ty_raw[g][:, t, :].bitcast(FP8), func=ACT.Copy, scale=tsc[:, g, t : t + 1]
            )

        widen_todo = [(g, t) for g in range(4) for t in range(4)]

        tx_codes = [keep.tile([LANES, P], U32, name=f"txc{g}", align_bytes=64) for g in range(4)]
        tx_scales = [keep.tile([LANES, P], U8, name=f"txs{g}", align_bytes=64) for g in range(4)]
        tx_bank, tx_il = {}, {}

        def tx_identity(g, s):
            bank = tpool.tile([LANES, 1024], BF16, name="tbank")
            for h in range(2):
                nc.tensor.matmul(
                    bank[:, 512 * h : 512 * h + 512],
                    ident_bf[:],
                    tx_raw[g][:, :, 256 * s + 128 * h : 256 * s + 128 * h + 128].rearrange("p t c -> p c t"),
                    start=True,
                    stop=True,
                )
            tx_bank[g, s] = bank

        def tx_empty(g, s):
            tile = three.tile([LANES, 1024], BF16, name="tx_il", align_bytes=64)
            nc.scalar.copy(out=tile[:], in_=tx_bank[g, s][:])
            tx_il[g, s] = tile

        def tx_direct(copy, g, s):
            tile = three.tile([LANES, 1024], BF16, name="tx_il", align_bytes=64)
            interleave(copy, tile[:], tx_raw[g][:, :, 256 * s : 256 * s + 256])
            tx_il[g, s] = tile

        def tx_quant(g, s):
            w = slice(256 * s, 256 * s + 256)
            quantize(tx_codes[g][:, w], tx_scales[g][:, w], tx_il[g, s][:])

        pool_todo = [(g, 256 * s + c, POOL_WIDTH) for g, s in TX_POOL for c in range(0, 256, POOL_WIDTH)]
        pool_ready = []

        def pool_il():
            g, c, n = pool_todo.pop(0)
            tile = keep.tile([LANES, 4 * POOL_WIDTH], BF16, name="gate", align_bytes=64)
            nc.gpsimd.tensor_scalar(
                out=tile[:].rearrange("p (c t) -> p c t", t=4),
                in0=tx_raw[g][:, :, c : c + n].rearrange("p t c -> p c t"),
                scalar1=1.0,
                scalar2=0.0,
                op0=ALU.mult,
                op1=ALU.add,
            )
            pool_ready.append((g, c, n, tile))

        def pool_quant():
            g, c, n, tile = pool_ready.pop(0)
            quantize(tx_codes[g][:, c : c + n], tx_scales[g][:, c : c + n], tile[:])

        transposes(0)
        transposes(1)
        empty(0)
        later = {0: [("tx", 0)], 1: [("ty", 1)], 2: [("tx", 1)], 3: [("tx", 2)], 4: [("ty", 2)], 5: [("ty", 3)]}
        pe_tx = dict(zip(PE_STEPS, [(g, s) for g in range(4) for s in range(4) if (g, s) not in TX_POOL]))
        quant_due = []
        for i in range(STEPS):
            if i + XY_AHEAD < STEPS:
                load_xy(i + XY_AHEAD)
            for kind, g in later.get(i, ()):
                if kind == "ty":
                    load_ty(g)
                else:
                    load_tx(g)
            if i == TX3_STEP:
                load_tx(3)
            quant1(i)
            if i + 2 < STEPS:
                transposes(i + 2)
            mm1(i)
            if i in pe_tx:
                tx_identity(*pe_tx[i])
            if i + 1 < STEPS:
                empty(i + 1)
            if i >= 1:
                cross(i - 1)
            if i - 1 in pe_tx:
                tx_empty(*pe_tx[i - 1])
                quant_due.append(pe_tx[i - 1])
            g, k = divmod(i - 5, 4)
            if g >= 0:
                flux_il(g, k)
            if pool_ready:
                pool_quant()
            if i >= POOL_START and pool_todo:
                pool_il()
            if i >= 1:
                flux_step(i - 1)
            if g >= 0:
                flux_q(g, k)
            if len(quant_due) > 1:
                tx_quant(*quant_due.pop(0))
            if i in WIDEN_STEPS:
                widen(*widen_todo.pop(0))
        if pool_ready:
            pool_quant()
        cross(STEPS - 1)

        ty_il, codes2, obank = {}, {}, {}

        def il_slice(j):
            g, s = divmod(j, 4)
            ty_il[j] = four.tile([LANES, 1024], BF16, name="ty_il", align_bytes=64)
            copy = nc.scalar.copy if j in SCALAR_TY else nc.vector.tensor_copy
            interleave(copy, ty_il[j][:], wide[g][:, :, 256 * s : 256 * s + 256])

        def quant2(j):
            c = four.tile([LANES, 256], U32, name="codes2", align_bytes=64)
            s = four.tile([LANES, 256], U8, name="scales2", align_bytes=64)
            quantize(c[:], s[:], ty_il[j][:])
            codes2[j] = (c, s)

        def mm2(j):
            g, s = divmod(j, 4)
            for h in range(2):
                p = 2 * s + h
                if g == 0:
                    if p < 4:
                        obank[p] = tpool.tile([LANES, R], F32, name="tbank")
                    else:
                        obank[p] = gpool.tile([LANES, R], F32, name="gbank")
                for side in range(2):
                    c, sc = (tx_codes[g], tx_scales[g]) if side == 0 else codes2[j]
                    w = slice(128 * p, 128 * p + 128) if side == 0 else slice(128 * h, 128 * h + 128)
                    fc, fs = fcodes[g, side]
                    nc.tensor.matmul_mx(
                        out=obank[p][:],
                        lhsT=c[:, w].bitcast(FP8X4),
                        lhsT_scale=sc[:, w],
                        rhs=fc[:].bitcast(FP8X4),
                        rhs_scale=fs[:],
                        start=(g == 0 and side == 0),
                        stop=(g == 3 and side == 1),
                    )

        res = {}

        def finish(p):
            if p % 2 == 0:
                res[p // 2] = xyp.tile([LANES, 2, R], F32, name="xy")
            t = res[p // 2]
            if p in VECTOR_OUT:
                nc.vector.tensor_copy(out=t[:, p % 2, :], in_=obank[p][:])
            else:
                nc.scalar.copy(out=t[:, p % 2, :], in_=obank[p][:])
            nc.sync.dma_start(out=out[128 * p : 128 * p + 128, :], in_=t[:, p % 2, :])

        late_flux = [(2, 3), (3, 0), (3, 1), (3, 2), (3, 3)]
        for n in range(EARLY_W):
            widen(*widen_todo.pop(0))
        if 0 in SCALAR_TY:
            il_slice(0)
        flux_step(STEPS - 1)
        direct = [(g, s) for g in range(4) for s in range(4) if (g, s) not in TX_POOL and (g, s) not in pe_tx.values()]
        slots = 17
        for j in range(slots):
            if quant_due:
                tx_quant(*quant_due.pop(0))
            if j == 0 and 0 not in SCALAR_TY:
                il_slice(0)
            elif j < 16 and j not in SCALAR_TY:
                il_slice(j)
            if j + 1 < 16 and j + 1 in SCALAR_TY:
                il_slice(j + 1)
            if j < 16:
                if (j // 4, j % 4) in direct:
                    tx_direct(nc.vector.tensor_copy, j // 4, j % 4)
                if j < len(late_flux):
                    flux_il(*late_flux[j])
            if pool_todo or pool_ready:
                if pool_ready:
                    pool_quant()
                if pool_todo:
                    pool_il()
            if j < LATE_W and widen_todo:
                widen(*widen_todo.pop(0))
            if j >= 1:
                quant2(j - 1)
                if ((j - 1) // 4, (j - 1) % 4) in direct:
                    tx_quant((j - 1) // 4, (j - 1) % 4)
                mm2(j - 1)
            if j < len(late_flux):
                flux_q(*late_flux[j])
            if j - 1 >= 12:
                finish(2 * (j - 13))
                finish(2 * (j - 13) + 1)
